import numpy as np
import ml_dtypes


def mxq(x, axis, fmt="e4m3"):
    dtype, down = {"e4m3": (ml_dtypes.float8_e4m3fn, 7), "e5m2": (ml_dtypes.float8_e5m2, 14)}[fmt]
    v = np.moveaxis(np.asarray(x, np.float32).astype(ml_dtypes.bfloat16).astype(np.float64), axis, -1)
    blocks = v.reshape(v.shape[:-1] + (-1, 32))
    amax = np.abs(blocks).max(-1, keepdims=True)
    byte = np.maximum(np.where(amax > 0, np.frexp(amax)[1] - 1 + 127, 0) - down, 1)
    scale = np.exp2(byte - 127.0)
    codes = (blocks / scale).astype(np.float32).astype(dtype).astype(np.float64)
    return np.moveaxis((codes * scale).reshape(v.shape), -1, axis)


WIDE = False


def mx_kscale(k):
    if not WIDE:
        return np.ones(k)
    levels = np.array([10, -10, 5, -5, 0])
    if k % 512:
        return np.exp2(np.random.permutation(np.resize(levels, k // 32))).repeat(32)
    a = np.empty((k // 512, 16))
    for p in range(k // 512):
        a[p, :8] = np.random.permutation(np.resize(levels, 8))
        for g in range(8):
            far = levels[np.abs(levels - a[p, g]) >= 10]
            a[p, g + 8] = far[np.random.randint(len(far))]
    return np.exp2(a.ravel()).repeat(32)


def f64(x):
    return np.asarray(x).astype(np.float64)


def striped(idx):
    return np.tile(np.asarray(idx).reshape(-1, 16).T, (8, 1)).astype(np.uint16)


def unstriped(offs):
    return offs[:16].T.reshape(-1).astype(np.int64)


E2M1 = np.array([0.0, 0.5, 1.0, 1.5, 2.0, 3.0, 4.0, 6.0, -0.0, -0.5, -1.0, -1.5, -2.0, -3.0, -4.0, -6.0])


def pack_weight(w, fmt):
    k, n = w.shape
    w = f64(np.asarray(w, np.float32).astype(ml_dtypes.bfloat16)).reshape(k // 32, 32, n)
    amax = np.abs(w).max(1)
    if fmt == "e4m3":
        byte = np.frexp(amax)[1] - 1 + 127 - 7
    else:
        mant, ex = np.frexp(amax / 6.0)
        byte = np.where(mant > 0.5, ex, ex - 1) + 127
    byte = np.clip(np.where(amax > 0, byte, 1), 1, 254)
    scaled = (w * np.exp2(127.0 - byte)[:, None, :]).reshape(k, n).astype(np.float32)
    by_word = np.ascontiguousarray(scaled.reshape(k // 512, 128, 4, n).transpose(0, 1, 3, 2))
    if fmt == "e4m3":
        words = by_word.astype(ml_dtypes.float8_e4m3fn).view(np.uint8)
    else:
        c = by_word.astype(ml_dtypes.float4_e2m1fn).view(np.uint8) & 0xF
        words = (c[..., 0::2] | (c[..., 1::2] << 4)).reshape(k // 512, 128, 2 * n)
    return np.ascontiguousarray(words), np.ascontiguousarray(byte.astype(np.uint8).reshape(k // 512, 16, n))


def unpack_weight(words, scales, fmt):
    g, _, n = scales.shape
    words = np.ascontiguousarray(words).reshape(g, 128, n, -1)
    if fmt == "e4m3":
        vals = words.view(ml_dtypes.float8_e4m3fn).astype(np.float64)
    else:
        nib = np.empty((g, 128, n, 4), np.uint8)
        nib[..., 0::2] = words & 0xF
        nib[..., 1::2] = words >> 4
        vals = E2M1[nib]
    vals = vals * np.repeat(np.exp2(scales.astype(np.float64) - 127.0), 8, axis=1)[..., None]
    return vals.transpose(0, 1, 3, 2).reshape(g * 512, n)


def sigmoid(v):
    return 1.0 / (1.0 + np.exp(-v))


def bf(x):
    return np.asarray(x, np.float32).astype(ml_dtypes.bfloat16)


def planes(Y):
    r, m = Y.shape
    b = f64(bf(Y)).reshape(r // 32, 32, m)
    amax = np.abs(b).max(1)
    byte = np.clip(np.where(amax > 0, np.frexp(amax)[1] - 1 + 127 - 7, 1), 1, 254)
    codes = (b * np.exp2(127.0 - byte)[:, None, :]).reshape(r, m).astype(np.float32).astype(ml_dtypes.float8_e4m3fn).view(np.uint8)
    words = codes.reshape(r // 512, 128, 4, m).transpose(0, 1, 3, 2)
    return np.ascontiguousarray(words), np.ascontiguousarray(byte.astype(np.uint8).reshape(r // 512, 16, m))


D, T, I, Q, E, G, M = 512, 2048, 512, 256, 512, 64, 1024


def setup_inputs():
    n = np.random.standard_normal
    idx = np.random.permutation(T)[:I]
    idx2 = np.random.permutation(M)[:Q]
    fd = mx_kscale(D)
    fi = mx_kscale(I)
    ti = np.ones(T)
    ti[idx] = fi
    keysp = pack_weight(n((D, T)) / fd[:, None], "e2m1")
    return {
        "query": (n((D, Q)) * 1.2 / np.sqrt(D) * fd[:, None]).astype(np.float32),
        "keys_words": keysp[0],
        "keys_scales": keysp[1],
        "guess": np.tile(np.random.uniform(0.05, 0.3, T), (128, 1)).astype(np.float32),
        "steep": np.tile(np.random.uniform(1.0, 3.0, T), (128, 1)).astype(np.float32),
        "thr": np.tile(np.random.uniform(-0.5, 1.0, T), (128, 1)).astype(np.float32),
        "lam": (np.random.uniform(0.6, 1.5, (Q, 1))).astype(np.float32),
        "mix": (np.random.uniform(0.2, 0.8, (Q, 1))).astype(np.float32),
        "os": (np.random.uniform(4.0, 16.0, (1, I)) * fi).astype(np.float32),
        "vals": (n((E, T)) / ti).astype(np.float32),
        "member": (n((E, M))).astype(np.float32),
        "mgain": np.tile(np.random.uniform(0.5, 2.0, M), (128, 1)).astype(np.float32),
        "offs": striped(idx),
        "offs2": striped(idx2),
    }


def reference(query, keys_words, keys_scales, guess, steep, thr, lam, mix, os, vals, member, mgain, offs, offs2):
    idx = unstriped(offs)
    idx2 = unstriped(offs2)
    keysu = unpack_weight(keys_words, keys_scales, "e2m1")
    queryq = mxq(f64(query), 0, "e4m3")
    keysidxg = keysu[:, idx]
    a = queryq.T @ keysidxg
    sg = sigmoid((a - f64(thr)[:1][:, idx]) * f64(steep)[:1][:, idx])
    s = np.log(sg * (1.0 - f64(guess)[:1][:, idx]) + f64(guess)[:1][:, idx]) * f64(lam)
    p = np.exp(s - np.max(s, axis=1, keepdims=True))
    r = p / np.sum(p, axis=1, keepdims=True)
    pm = r.reshape(Q, G, I // G).mean(axis=2)
    pr = np.repeat(pm, I // G, axis=1)
    w = r * (1.0 - f64(mix)) + pr * f64(mix)
    wo1 = w * f64(os)
    wt1 = wo1.T
    vt1 = f64(vals)[:, idx].T
    vt1q = mxq(vt1, 0, "e4m3")
    wt1q = mxq(wt1, 0, "e4m3")
    o = vt1q.T @ wt1q
    y = o * f64(mgain)[:1][:, idx2] + f64(member)[:, idx2]
    words, scales = planes(y)
    return y, words, scales

@@ -1,0 +1,247 @@
+from contextlib import ExitStack
+
+import concourse.mybir as mybir
+from concourse.masks import make_identity
+
+D, T, I, Q, E, M = 512, 2048, 512, 256, 512, 1024
+RUN = 8
+G = I // RUN
+P = 128
+PACK = 4
+QT = Q // P
+LIVE = 96
+
+FLOPS = 2 * D * Q * I + 2 * I * E * Q
+
+F32 = mybir.dt.float32
+BF16 = mybir.dt.bfloat16
+I32 = mybir.dt.int32
+U32 = mybir.dt.uint32
+U16 = mybir.dt.uint16
+U8 = mybir.dt.uint8
+FP8X4 = mybir.dt.float8_e4m3fn_x4
+FP4X4 = mybir.dt.float4_e2m1fn_x4
+ALU = mybir.AluOpType
+ACT = mybir.ActivationFunctionType
+AX = mybir.AxisListType
+
+
+def tile_attend_answerodds_smoothpage_bymember_pl_kernel(
+    tc, query, keys_words, keys_scales, guess, steep, thr, lam, mix, slot_factor, vals, member, mgain, offs, offs2,
+    out_0, out_1, out_2,
+):
+    nc = tc.nc
+    with ExitStack() as ctx:
+        sb = ctx.enter_context(tc.tile_pool(name="sb", bufs=1))
+        ps = ctx.enter_context(tc.psum_pool(name="ps", bufs=1))
+
+        def tile(name, shape, dtype):
+            return sb.tile(shape, dtype, name=name, align_bytes=64)
+
+        def bank(tag, name, shape):
+            return ps.tile(shape, F32, name=name, tag=tag)
+
+        slots = tile("slots", [P, I // 16], U16)
+        picks = tile("picks", [P, Q // 16], U16)
+        key_pool = tile("key_pool", [P, T], U16)
+        key_scale_pool = tile("key_scale_pool", [P, T], U8)
+        thr_pool = tile("thr_pool", [P, T], F32)
+        steep_pool = tile("steep_pool", [P, T], F32)
+        guess_pool = tile("guess_pool", [P, T], F32)
+        q_raw = tile("q_raw", [P, PACK, Q], F32)
+        val_pool = [tile("val_pool%d" % j, [P, T], F32) for j in range(PACK)]
+        member_pool = [tile("member_pool%d" % j, [P, M], F32) for j in range(PACK)]
+        gain_pool = tile("gain_pool", [P, M], F32)
+        lam_col = tile("lam_col", [P, QT], F32)
+        mix_col = tile("mix_col", [P, QT], F32)
+        os_col = tile("os_col", [P, PACK], F32)
+        ident = tile("ident", [P, P], F32)
+
+        nc.gpsimd.memset(key_scale_pool[:].bitcast(I32), 0)
+        make_identity(nc, ident[:])
+        for pool in (thr_pool, steep_pool, guess_pool):
+            nc.vector.memset(pool[0:LIVE, :], 0.0)
+
+        val_planes = vals.rearrange("(m j) t -> j m t", j=PACK)
+        member_planes = member.rearrange("(m j) n -> j m n", j=PACK)
+        scale_rows = keys_scales[0].bitcast(I32).rearrange("(b r) n -> r b n", r=PACK)
+
+        nc.sync.dma_start(slots[:], offs)
+        nc.sync.dma_start(key_pool[:].bitcast(I32), keys_words[0].bitcast(I32))
+        for r in range(PACK):
+            nc.sync.dma_start(key_scale_pool[r:P:32, :].bitcast(I32), scale_rows[r])
+        nc.sync.dma_start(thr_pool[LIVE:P, :], thr[LIVE:P, :])
+        nc.sync.dma_start(steep_pool[LIVE:P, :], steep[LIVE:P, :])
+        nc.sync.dma_start(q_raw[:], query.rearrange("(p j) q -> p j q", j=PACK))
+        nc.sync.dma_start(val_pool[0][:], val_planes[0])
+        nc.sync.dma_start(guess_pool[LIVE:P, :], guess[LIVE:P, :])
+        for j in range(1, PACK):
+            nc.sync.dma_start(val_pool[j][:], val_planes[j])
+        with nc.allow_non_contiguous_dma(reason="one factor a query row, one row a partition"):
+            nc.sync.dma_start(lam_col[:], lam.rearrange("(h p) o -> p (h o)", p=P))
+            nc.sync.dma_start(mix_col[:], mix.rearrange("(h p) o -> p (h o)", p=P))
+        nc.sync.dma_start(os_col[:], slot_factor.rearrange("o (p t) -> p (o t)", t=PACK))
+        nc.sync.dma_start(picks[:], offs2)
+        nc.sync.dma_start(gain_pool[:], mgain)
+        for j in range(PACK):
+            nc.sync.dma_start(member_pool[j][:], member_planes[j])
+
+        key_words = tile("key_words", [P, I], U16)
+        key_scales = tile("key_scales", [P, I], U8)
+        nc.vector.tensor_copy(key_words[:], key_pool[:].indirect(slots[:]))
+        nc.vector.tensor_copy(key_scales[:], key_scale_pool[:].indirect(slots[:]))
+
+        q_bf = tile("q_bf", [P, Q, PACK], BF16)
+        q_codes = tile("q_codes", [P, Q], U32)
+        q_scales = tile("q_scales", [P, Q], U8)
+        nc.vector.tensor_copy(q_bf[:], q_raw[:].rearrange("p j q -> p q j"))
+        nc.vector.quantize_mx(q_codes[:].bitcast(FP8X4), q_scales[:], q_bf[:].rearrange("p q j -> p (q j)"))
+
+        thr_row = tile("thr_row", [P, I], F32)
+        steep_row = tile("steep_row", [P, I], F32)
+        guess_row = tile("guess_row", [P, I], F32)
+        nc.scalar.activation(thr_row[:], thr_pool[:].indirect(slots[:]), ACT.Copy)
+        nc.scalar.activation(steep_row[:], steep_pool[:].indirect(slots[:]), ACT.Copy)
+        thr_ps = bank("c0", "thr_ps", [P, PACK, P])
+        steep_ps = bank("c1", "steep_ps", [P, PACK, P])
+        for row, turned in ((thr_row, thr_ps), (steep_row, steep_ps)):
+            for c in range(PACK):
+                nc.tensor.transpose(turned[:, c, :], row[:, c * P : (c + 1) * P], ident[:])
+        steep_col = tile("steep_col", [P, PACK], F32)
+        shift_col = tile("shift_col", [P, PACK], F32)
+        nc.vector.tensor_copy(steep_col[:], steep_ps[:, :, LIVE])
+        nc.vector.scalar_tensor_tensor(shift_col[:], thr_ps[:, :, LIVE], -1.0, steep_col[:], ALU.mult, ALU.mult)
+
+        nc.vector.tensor_copy(guess_row[:], guess_pool[:].indirect(slots[:]))
+
+        score_ps = [bank("a%d" % h, "score_ps%d" % h, [P, 2, Q]) for h in range(2)]
+        for c in range(PACK):
+            cols = slice(c * P, (c + 1) * P)
+            nc.tensor.matmul_mx(
+                score_ps[c // 2][:, c % 2, :],
+                lhsT=key_words[:, cols].bitcast(FP4X4), lhsT_scale=key_scales[:, cols],
+                rhs=q_codes[:].bitcast(FP8X4), rhs_scale=q_scales[:], start=True, stop=True,
+            )
+        sg = tile("sg", [P, PACK, Q], F32)
+        for c in range(PACK):
+            nc.scalar.activation(
+                sg[:, c, :], score_ps[c // 2][:, c % 2, :], ACT.Sigmoid,
+                bias=shift_col[:, c : c + 1], scale=steep_col[:, c : c + 1],
+            )
+
+        guess_ps = bank("c0", "guess_ps", [P, PACK, P])
+        for c in range(PACK):
+            nc.tensor.transpose(guess_ps[:, c, :], guess_row[:, c * P : (c + 1) * P], ident[:])
+        guess_col = tile("guess_col", [P, PACK], F32)
+        rest_col = tile("rest_col", [P, PACK], F32)
+        nc.vector.tensor_copy(guess_col[:], guess_ps[:, :, LIVE])
+        nc.vector.tensor_scalar(rest_col[:], guess_ps[:, :, LIVE], -1.0, 1.0, ALU.mult, ALU.add)
+
+        log_chance = tile("log_chance", [P, PACK, Q], F32)
+        for c in range(PACK):
+            nc.scalar.activation(
+                log_chance[:, c, :], sg[:, c, :], ACT.Ln,
+                bias=guess_col[:, c : c + 1], scale=rest_col[:, c : c + 1],
+            )
+
+        v_bf = tile("v_bf", [P, PACK, P, PACK], BF16)
+        v_codes = tile("v_codes", [P, E], U32)
+        v_scales = tile("v_scales", [P, E], U8)
+        v_words = v_bf[:].rearrange("p j m t -> p j (m t)").bitcast(F32).rearrange("p j (m u) -> p j m u", u=2)
+        for j in range(PACK):
+            picked = tile("val_picked%d" % j, [P, I], BF16)
+            nc.vector.tensor_copy(picked[:], val_pool[j][:].indirect(slots[:]))
+            pairs = picked[:].bitcast(F32)
+            turned = bank("d%d" % (j % 2), "val_turned%d" % j, [P, 2, P])
+            for u in range(2):
+                nc.tensor.transpose(turned[:, u, :], pairs[:, u : I // 2 : 2], ident[:])
+            nc.scalar.copy(v_words[:, j], turned[:].rearrange("p u m -> p m u"))
+            cols = slice(j * P, (j + 1) * P)
+            nc.vector.quantize_mx(
+                v_codes[:, cols].bitcast(FP8X4), v_scales[:, cols], v_bf[:, j].rearrange("p m t -> p (m t)")
+            )
+
+        neg_lam = tile("neg_lam", [P, QT], F32)
+        shares = tile("shares", [P, QT, 2], F32)
+        nc.vector.tensor_scalar(neg_lam[:], lam_col[:], -1.0, None, ALU.mult)
+        nc.vector.tensor_scalar(shares[:, :, 0], mix_col[:], -1.0, 1.0, ALU.mult, ALU.add)
+        nc.vector.tensor_scalar(shares[:, :, 1], mix_col[:], 1.0 / RUN, None, ALU.mult)
+
+        neg_s, neg_max, p, total = [], [], [], []
+        for h in range(QT):
+            turned = bank("b%d" % h, "log_turned%d" % h, [P, I])
+            for c in range(PACK):
+                nc.tensor.transpose(turned[:, c * P : (c + 1) * P], log_chance[:, c, h * P : (h + 1) * P], ident[:])
+            neg_s.append(tile("neg_s%d" % h, [P, PACK, P], F32))
+            neg_max.append(tile("neg_max%d" % h, [P, 1], F32))
+            nc.vector.tensor_scalar(
+                neg_s[h][:], turned[:].rearrange("p (s t) -> p t s", t=PACK), neg_lam[:, h : h + 1], None,
+                ALU.mult, ALU.min, accum_out=neg_max[h][:],
+            )
+        for h in range(QT):
+            p.append(tile("p%d" % h, [P, PACK, P], F32))
+            total.append(tile("total%d" % h, [P, 1], F32))
+            nc.scalar.activation(p[h][:], neg_s[h][:], ACT.Exp, bias=neg_max[h][:], scale=-1.0, accum_out=total[h][:])
+
+        gain = tile("gain", [P, Q], F32)
+        member_cols = tile("member_cols", [P, PACK, Q], F32)
+        nc.scalar.activation(gain[:], gain_pool[:].indirect(picks[:]), ACT.Copy)
+        for j in range(PACK):
+            nc.scalar.activation(member_cols[:, j, :], member_pool[j][:].indirect(picks[:]), ACT.Copy)
+
+        w_codes, w_scales = [], []
+        for h in range(QT):
+            run_sum = tile("run_sum%d" % h, [P, G], F32)
+            nc.vector.tensor_reduce(run_sum[:], p[h][:].rearrange("p t (g k) -> p g t k", k=2), AX.XY, ALU.add)
+            inv = tile("inv%d" % h, [P, 1], F32)
+            nc.vector.reciprocal(inv[:], total[h][:])
+            factor = tile("factor%d" % h, [P, 2], F32)
+            nc.vector.tensor_scalar(factor[:], shares[:, h, :], inv[:], None, ALU.mult)
+            run_term = tile("run_term%d" % h, [P, G, 2], F32)
+            nc.vector.tensor_scalar(
+                run_term[:], run_sum[:].unsqueeze(2).broadcast_to([P, G, 2]), factor[:, 1:2], None, ALU.mult
+            )
+            w = tile("w%d" % h, [P, PACK, P], F32)
+            nc.vector.scalar_tensor_tensor(
+                w[:], p[h][:], factor[:, 0:1],
+                run_term[:].rearrange("p g k -> p (g k)").unsqueeze(1).broadcast_to([P, PACK, P]),
+                ALU.mult, ALU.add,
+            )
+            turned = bank("a%d" % h, "w_turned%d" % h, [P, PACK, P])
+            for t in range(PACK):
+                nc.tensor.transpose(turned[:, t, :], w[:, t, :], ident[:])
+            w_bf = tile("w_bf%d" % h, [P, P, PACK], BF16)
+            nc.vector.tensor_tensor(
+                w_bf[:], turned[:].rearrange("p t q -> p q t"),
+                os_col[:].unsqueeze(1).broadcast_to([P, P, PACK]), ALU.mult,
+            )
+            w_codes.append(tile("w_codes%d" % h, [P, P], U32))
+            w_scales.append(tile("w_scales%d" % h, [P, P], U8))
+            nc.vector.quantize_mx(w_codes[h][:].bitcast(FP8X4), w_scales[h][:], w_bf[:].rearrange("p q t -> p (q t)"))
+
+        y_codes = tile("y_codes", [P, Q], U32)
+        y_scales = tile("y_scales", [P, Q], U8)
+        y_rows = out_0.rearrange("(m j) q -> m j q", j=PACK)
+        for h in range(QT):
+            q_cols = slice(h * P, (h + 1) * P)
+            o_ps = bank("b%d" % h, "o_ps%d" % h, [P, PACK, P])
+            for j in range(PACK):
+                cols = slice(j * P, (j + 1) * P)
+                nc.tensor.matmul_mx(
+                    o_ps[:, j, :], lhsT=v_codes[:, cols].bitcast(FP8X4), lhsT_scale=v_scales[:, cols],
+                    rhs=w_codes[h][:].bitcast(FP8X4), rhs_scale=w_scales[h][:], start=True, stop=True,
+                )
+            scaled = tile("scaled%d" % h, [P, PACK, P], F32)
+            nc.vector.tensor_tensor(scaled[:], o_ps[:], gain[:, q_cols].unsqueeze(1).broadcast_to([P, PACK, P]), ALU.mult)
+            y = tile("y%d" % h, [P, PACK, P], F32)
+            nc.vector.tensor_tensor(y[:], scaled[:], member_cols[:, :, q_cols], ALU.add)
+            nc.sync.dma_start(y_rows[:, :, q_cols], y[:])
+            y_bf = tile("y_bf%d" % h, [P, P, PACK], BF16)
+            nc.scalar.copy(y_bf[:], y[:].rearrange("p j q -> p q j"))
+            nc.vector.quantize_mx(y_codes[:, q_cols].bitcast(FP8X4), y_scales[:, q_cols], y_bf[:].rearrange("p q j -> p (q j)"))
+
+        nc.sync.dma_start(out_1[0].rearrange("p c r -> p (c r)").bitcast(I32), y_codes[:].bitcast(I32))
+        out_scale_rows = out_2[0].bitcast(I32).rearrange("(b r) n -> r b n", r=PACK)
+        for r in range(PACK):
+            queue = nc.scalar if r % 2 else nc.sync
+            queue.dma_start(out_scale_rows[r], y_scales[r:P:32, :].bitcast(I32))

@@ -35,8 +35,8 @@ def tile_attend_answerodds_smoothpage_bymember_pl_kernel(
         sb = ctx.enter_context(tc.tile_pool(name="sb", bufs=1))
         ps = ctx.enter_context(tc.psum_pool(name="ps", bufs=1))
 
-        def tile(name, shape, dtype):
-            return sb.tile(shape, dtype, name=name, align_bytes=64)
+        def tile(name, shape, dtype, tag=""):
+            return sb.tile(shape, dtype, name=name, tag=tag or name, align_bytes=64)
 
         def bank(tag, name, shape):
             return ps.tile(shape, F32, name=name, tag=tag)
@@ -58,6 +58,10 @@ def tile_attend_answerodds_smoothpage_bymember_pl_kernel(
         ident = tile("ident", [P, P], F32)
 
         nc.gpsimd.memset(key_scale_pool[:].bitcast(I32), 0)
+        warm_in = tile("warm_in", [P, 1], F32)
+        warm_out = tile("warm_out", [P, 1], F32)
+        nc.gpsimd.memset(warm_in[:], 0.0)
+        nc.scalar.activation(warm_out[:], warm_in[:], ACT.Sigmoid)
         make_identity(nc, ident[:])
         for pool in (thr_pool, steep_pool, guess_pool):
             nc.vector.memset(pool[0:LIVE, :], 0.0)
@@ -67,21 +71,22 @@ def tile_attend_answerodds_smoothpage_bymember_pl_kernel(
         scale_rows = keys_scales[0].bitcast(I32).rearrange("(b r) n -> r b n", r=PACK)
 
         nc.sync.dma_start(slots[:], offs)
+        nc.sync.dma_start(picks[:], offs2)
+        nc.sync.dma_start(os_col[:], slot_factor.rearrange("o (p t) -> p (o t)", t=PACK))
         nc.sync.dma_start(key_pool[:].bitcast(I32), keys_words[0].bitcast(I32))
         for r in range(PACK):
             nc.sync.dma_start(key_scale_pool[r:P:32, :].bitcast(I32), scale_rows[r])
         nc.sync.dma_start(thr_pool[LIVE:P, :], thr[LIVE:P, :])
-        nc.sync.dma_start(steep_pool[LIVE:P, :], steep[LIVE:P, :])
         nc.sync.dma_start(q_raw[:], query.rearrange("(p j) q -> p j q", j=PACK))
-        nc.sync.dma_start(val_pool[0][:], val_planes[0])
+        nc.sync.dma_start(steep_pool[LIVE:P, :], steep[LIVE:P, :])
         nc.sync.dma_start(guess_pool[LIVE:P, :], guess[LIVE:P, :])
-        for j in range(1, PACK):
-            nc.sync.dma_start(val_pool[j][:], val_planes[j])
+        nc.sync.dma_start(val_pool[0][:], val_planes[0])
+        nc.sync.dma_start(val_pool[1][:], val_planes[1])
         with nc.allow_non_contiguous_dma(reason="one factor a query row, one row a partition"):
             nc.sync.dma_start(lam_col[:], lam.rearrange("(h p) o -> p (h o)", p=P))
             nc.sync.dma_start(mix_col[:], mix.rearrange("(h p) o -> p (h o)", p=P))
-        nc.sync.dma_start(os_col[:], slot_factor.rearrange("o (p t) -> p (o t)", t=PACK))
-        nc.sync.dma_start(picks[:], offs2)
+        for j in range(2, PACK):
+            nc.sync.dma_start(val_pool[j][:], val_planes[j])
         nc.sync.dma_start(gain_pool[:], mgain)
         for j in range(PACK):
             nc.sync.dma_start(member_pool[j][:], member_planes[j])
@@ -99,9 +104,10 @@ def tile_attend_answerodds_smoothpage_bymember_pl_kernel(
 
         thr_row = tile("thr_row", [P, I], F32)
         steep_row = tile("steep_row", [P, I], F32)
-        guess_row = tile("guess_row", [P, I], F32)
-        nc.scalar.activation(thr_row[:], thr_pool[:].indirect(slots[:]), ACT.Copy)
+        guess_row = tile("guess_row", [P, I], F32, tag="key_scale_pool")
+        nc.scalar.activation(thr_row[:], thr_pool[:].indirect(slots[:]), ACT.Copy, scale=-1.0)
         nc.scalar.activation(steep_row[:], steep_pool[:].indirect(slots[:]), ACT.Copy)
+        nc.vector.tensor_copy(guess_row[:], guess_pool[:].indirect(slots[:]))
         thr_ps = bank("c0", "thr_ps", [P, PACK, P])
         steep_ps = bank("c1", "steep_ps", [P, PACK, P])
         for row, turned in ((thr_row, thr_ps), (steep_row, steep_ps)):
@@ -109,10 +115,12 @@ def tile_attend_answerodds_smoothpage_bymember_pl_kernel(
                 nc.tensor.transpose(turned[:, c, :], row[:, c * P : (c + 1) * P], ident[:])
         steep_col = tile("steep_col", [P, PACK], F32)
         shift_col = tile("shift_col", [P, PACK], F32)
-        nc.vector.tensor_copy(steep_col[:], steep_ps[:, :, LIVE])
-        nc.vector.scalar_tensor_tensor(shift_col[:], thr_ps[:, :, LIVE], -1.0, steep_col[:], ALU.mult, ALU.mult)
+        nc.scalar.copy(steep_col[:], steep_ps[:, :, LIVE])
+        for c in range(PACK):
+            nc.scalar.activation(
+                shift_col[:, c : c + 1], thr_ps[:, c, LIVE : LIVE + 1], ACT.Copy, scale=steep_col[:, c : c + 1]
+            )
 
-        nc.vector.tensor_copy(guess_row[:], guess_pool[:].indirect(slots[:]))
 
         score_ps = [bank("a%d" % h, "score_ps%d" % h, [P, 2, Q]) for h in range(2)]
         for c in range(PACK):
@@ -129,13 +137,30 @@ def tile_attend_answerodds_smoothpage_bymember_pl_kernel(
                 bias=shift_col[:, c : c + 1], scale=steep_col[:, c : c + 1],
             )
 
-        guess_ps = bank("c0", "guess_ps", [P, PACK, P])
+        turn_ps = [bank("d%d" % h, "turn_ps%d" % h, [P, I]) for h in range(QT)]
+        third_ps = bank("b0", "third_ps", [P, I])
+        val_turned = [
+            ps_tile[:, : 2 * P].rearrange("p (u m) -> p u m", u=2) for ps_tile in (turn_ps[0], turn_ps[1], third_ps, turn_ps[0])
+        ]
+
+        def gather_values(j):
+            picked = tile("val_picked%d" % j, [P, I], BF16, tag=("guess_pool", "val_picked1", "val_picked2", "val_picked3")[j])
+            nc.vector.tensor_copy(picked[:], val_pool[j][:].indirect(slots[:]))
+            return picked
+
+        def turn_values(j, picked):
+            pairs = picked[:].bitcast(F32)
+            for u in range(2):
+                nc.tensor.transpose(val_turned[j][:, u, :], pairs[:, u : I // 2 : 2], ident[:])
+
+        guess_ps = bank("b1", "guess_ps", [P, PACK, P])
         for c in range(PACK):
             nc.tensor.transpose(guess_ps[:, c, :], guess_row[:, c * P : (c + 1) * P], ident[:])
+        turn_values(0, gather_values(0))
         guess_col = tile("guess_col", [P, PACK], F32)
         rest_col = tile("rest_col", [P, PACK], F32)
-        nc.vector.tensor_copy(guess_col[:], guess_ps[:, :, LIVE])
-        nc.vector.tensor_scalar(rest_col[:], guess_ps[:, :, LIVE], -1.0, 1.0, ALU.mult, ALU.add)
+        nc.scalar.copy(guess_col[:], guess_ps[:, :, LIVE])
+        nc.scalar.activation(rest_col[:], guess_ps[:, :, LIVE], ACT.Copy, bias=1.0, scale=-1.0)
 
         log_chance = tile("log_chance", [P, PACK, Q], F32)
         for c in range(PACK):
@@ -144,52 +169,59 @@ def tile_attend_answerodds_smoothpage_bymember_pl_kernel(
                 bias=guess_col[:, c : c + 1], scale=rest_col[:, c : c + 1],
             )
 
-        v_bf = tile("v_bf", [P, PACK, P, PACK], BF16)
+        warm_out2 = tile("warm_out2", [P, 1], F32)
+        nc.scalar.activation(warm_out2[:], log_chance[:, PACK - 1, 0:1], ACT.Exp)
         v_codes = tile("v_codes", [P, E], U32)
         v_scales = tile("v_scales", [P, E], U8)
-        v_words = v_bf[:].rearrange("p j m t -> p j (m t)").bitcast(F32).rearrange("p j (m u) -> p j m u", u=2)
-        for j in range(PACK):
-            picked = tile("val_picked%d" % j, [P, I], BF16)
-            nc.vector.tensor_copy(picked[:], val_pool[j][:].indirect(slots[:]))
-            pairs = picked[:].bitcast(F32)
-            turned = bank("d%d" % (j % 2), "val_turned%d" % j, [P, 2, P])
-            for u in range(2):
-                nc.tensor.transpose(turned[:, u, :], pairs[:, u : I // 2 : 2], ident[:])
-            nc.scalar.copy(v_words[:, j], turned[:].rearrange("p u m -> p m u"))
+
+        def quantise_values(j, words):
             cols = slice(j * P, (j + 1) * P)
-            nc.vector.quantize_mx(
-                v_codes[:, cols].bitcast(FP8X4), v_scales[:, cols], v_bf[:, j].rearrange("p m t -> p (m t)")
-            )
+            nc.vector.quantize_mx(v_codes[:, cols].bitcast(FP8X4), v_scales[:, cols], words.bitcast(BF16))
+
+        def lay_values(j, words, copy):
+            copy(words.rearrange("p (m u) -> p m u", u=2), val_turned[j].rearrange("p u m -> p m u"))
+
+        v_words = [tile("v_words%d" % j, [P, 2 * P], F32)[:] for j in range(PACK - 1)] + [sg[:, PACK - 1, :]]
+        for j in range(1, PACK):
+            lay_values(j - 1, v_words[j - 1], nc.vector.tensor_copy)
+            last_picked = gather_values(j)
+            if j < PACK - 1:
+                turn_values(j, last_picked)
+            quantise_values(j - 1, v_words[j - 1])
 
         neg_lam = tile("neg_lam", [P, QT], F32)
         shares = tile("shares", [P, QT, 2], F32)
-        nc.vector.tensor_scalar(neg_lam[:], lam_col[:], -1.0, None, ALU.mult)
-        nc.vector.tensor_scalar(shares[:, :, 0], mix_col[:], -1.0, 1.0, ALU.mult, ALU.add)
-        nc.vector.tensor_scalar(shares[:, :, 1], mix_col[:], 1.0 / RUN, None, ALU.mult)
+        nc.gpsimd.tensor_scalar(neg_lam[:], lam_col[:], -1.0, 0.0, ALU.mult, ALU.add)
+        nc.gpsimd.tensor_scalar(shares[:, :, 0], mix_col[:], -1.0, 1.0, ALU.mult, ALU.add)
+        nc.gpsimd.tensor_scalar(shares[:, :, 1], mix_col[:], 1.0 / RUN, 0.0, ALU.mult, ALU.add)
 
-        neg_s, neg_max, p, total = [], [], [], []
+        p, total = [], []
+        stage = tile("stage", [P, PACK + 1, Q], F32)
+        neg_s = stage[:, :PACK, :].rearrange("p t (h s) -> p h t s", h=QT)
+        neg_max = [stage[:, PACK, h : h + 1] for h in range(QT)]
         for h in range(QT):
-            turned = bank("b%d" % h, "log_turned%d" % h, [P, I])
+            turned = turn_ps[h]
             for c in range(PACK):
                 nc.tensor.transpose(turned[:, c * P : (c + 1) * P], log_chance[:, c, h * P : (h + 1) * P], ident[:])
-            neg_s.append(tile("neg_s%d" % h, [P, PACK, P], F32))
-            neg_max.append(tile("neg_max%d" % h, [P, 1], F32))
             nc.vector.tensor_scalar(
-                neg_s[h][:], turned[:].rearrange("p (s t) -> p t s", t=PACK), neg_lam[:, h : h + 1], None,
-                ALU.mult, ALU.min, accum_out=neg_max[h][:],
+                neg_s[:, h], turned[:].rearrange("p (s t) -> p t s", t=PACK), neg_lam[:, h : h + 1], None,
+                ALU.mult, ALU.min, accum_out=neg_max[h],
             )
         for h in range(QT):
             p.append(tile("p%d" % h, [P, PACK, P], F32))
             total.append(tile("total%d" % h, [P, 1], F32))
-            nc.scalar.activation(p[h][:], neg_s[h][:], ACT.Exp, bias=neg_max[h][:], scale=-1.0, accum_out=total[h][:])
+            nc.scalar.activation(p[h][:], neg_s[:, h], ACT.Exp, bias=neg_max[h], scale=-1.0, accum_out=total[h][:])
 
-        gain = tile("gain", [P, Q], F32)
-        member_cols = tile("member_cols", [P, PACK, Q], F32)
-        nc.scalar.activation(gain[:], gain_pool[:].indirect(picks[:]), ACT.Copy)
+        turn_values(3, last_picked)
+        lay_values(3, v_words[3], nc.scalar.copy)
+
+        gain = stage[:, PACK, :]
+        member_cols = stage[:, :PACK, :]
+        nc.scalar.activation(gain, gain_pool[:].indirect(picks[:]), ACT.Copy)
         for j in range(PACK):
             nc.scalar.activation(member_cols[:, j, :], member_pool[j][:].indirect(picks[:]), ACT.Copy)
 
-        w_codes, w_scales = [], []
+        w_codes, w_scales, w_turned = [], [], []
         for h in range(QT):
             run_sum = tile("run_sum%d" % h, [P, G], F32)
             nc.vector.tensor_reduce(run_sum[:], p[h][:].rearrange("p t (g k) -> p g t k", k=2), AX.XY, ALU.add)
@@ -207,9 +239,12 @@ def tile_attend_answerodds_smoothpage_bymember_pl_kernel(
                 run_term[:].rearrange("p g k -> p (g k)").unsqueeze(1).broadcast_to([P, PACK, P]),
                 ALU.mult, ALU.add,
             )
-            turned = bank("a%d" % h, "w_turned%d" % h, [P, PACK, P])
+            w_turned.append(bank("a%d" % h, "w_turned%d" % h, [P, PACK, P]))
             for t in range(PACK):
-                nc.tensor.transpose(turned[:, t, :], w[:, t, :], ident[:])
+                nc.tensor.transpose(w_turned[h][:, t, :], w[:, t, :], ident[:])
+        quantise_values(3, v_words[3])
+        for h in range(QT):
+            turned = w_turned[h]
             w_bf = tile("w_bf%d" % h, [P, P, PACK], BF16)
             nc.vector.tensor_tensor(
                 w_bf[:], turned[:].rearrange("p t q -> p q t"),
@@ -224,7 +259,7 @@ def tile_attend_answerodds_smoothpage_bymember_pl_kernel(
         y_rows = out_0.rearrange("(m j) q -> m j q", j=PACK)
         for h in range(QT):
             q_cols = slice(h * P, (h + 1) * P)
-            o_ps = bank("b%d" % h, "o_ps%d" % h, [P, PACK, P])
+            o_ps = bank("c%d" % h, "o_ps%d" % h, [P, PACK, P])
             for j in range(PACK):
                 cols = slice(j * P, (j + 1) * P)
                 nc.tensor.matmul_mx(

@@ -71,22 +71,22 @@ def tile_attend_answerodds_smoothpage_bymember_pl_kernel(
         scale_rows = keys_scales[0].bitcast(I32).rearrange("(b r) n -> r b n", r=PACK)
 
         nc.sync.dma_start(slots[:], offs)
-        nc.sync.dma_start(picks[:], offs2)
-        nc.sync.dma_start(os_col[:], slot_factor.rearrange("o (p t) -> p (o t)", t=PACK))
+        nc.sync.dma_start(thr_pool[LIVE:P, :], thr[LIVE:P, :])
         nc.sync.dma_start(key_pool[:].bitcast(I32), keys_words[0].bitcast(I32))
         for r in range(PACK):
             nc.sync.dma_start(key_scale_pool[r:P:32, :].bitcast(I32), scale_rows[r])
-        nc.sync.dma_start(thr_pool[LIVE:P, :], thr[LIVE:P, :])
-        nc.sync.dma_start(q_raw[:], query.rearrange("(p j) q -> p j q", j=PACK))
         nc.sync.dma_start(steep_pool[LIVE:P, :], steep[LIVE:P, :])
+        nc.sync.dma_start(q_raw[:], query.rearrange("(p j) q -> p j q", j=PACK))
         nc.sync.dma_start(guess_pool[LIVE:P, :], guess[LIVE:P, :])
-        nc.sync.dma_start(val_pool[0][:], val_planes[0])
-        nc.sync.dma_start(val_pool[1][:], val_planes[1])
+        for j in range(2):
+            nc.sync.dma_start(val_pool[j][:], val_planes[j])
         with nc.allow_non_contiguous_dma(reason="one factor a query row, one row a partition"):
             nc.sync.dma_start(lam_col[:], lam.rearrange("(h p) o -> p (h o)", p=P))
             nc.sync.dma_start(mix_col[:], mix.rearrange("(h p) o -> p (h o)", p=P))
-        for j in range(2, PACK):
-            nc.sync.dma_start(val_pool[j][:], val_planes[j])
+        nc.sync.dma_start(val_pool[2][:], val_planes[2])
+        nc.sync.dma_start(os_col[:], slot_factor.rearrange("o (p t) -> p (o t)", t=PACK))
+        nc.sync.dma_start(picks[:], offs2)
+        nc.sync.dma_start(val_pool[3][:], val_planes[3])
         nc.sync.dma_start(gain_pool[:], mgain)
         for j in range(PACK):
             nc.sync.dma_start(member_pool[j][:], member_planes[j])
@@ -104,10 +104,9 @@ def tile_attend_answerodds_smoothpage_bymember_pl_kernel(
 
         thr_row = tile("thr_row", [P, I], F32)
         steep_row = tile("steep_row", [P, I], F32)
-        guess_row = tile("guess_row", [P, I], F32, tag="key_scale_pool")
+        guess_row = tile("guess_row", [P, I], F32)
         nc.scalar.activation(thr_row[:], thr_pool[:].indirect(slots[:]), ACT.Copy, scale=-1.0)
         nc.scalar.activation(steep_row[:], steep_pool[:].indirect(slots[:]), ACT.Copy)
-        nc.vector.tensor_copy(guess_row[:], guess_pool[:].indirect(slots[:]))
         thr_ps = bank("c0", "thr_ps", [P, PACK, P])
         steep_ps = bank("c1", "steep_ps", [P, PACK, P])
         for row, turned in ((thr_row, thr_ps), (steep_row, steep_ps)):
@@ -122,6 +121,8 @@ def tile_attend_answerodds_smoothpage_bymember_pl_kernel(
             )
 
 
+        nc.scalar.activation(guess_row[:], guess_pool[:].indirect(slots[:]), ACT.Copy)
+
         score_ps = [bank("a%d" % h, "score_ps%d" % h, [P, 2, Q]) for h in range(2)]
         for c in range(PACK):
             cols = slice(c * P, (c + 1) * P)
@@ -130,7 +131,7 @@ def tile_attend_answerodds_smoothpage_bymember_pl_kernel(
                 lhsT=key_words[:, cols].bitcast(FP4X4), lhsT_scale=key_scales[:, cols],
                 rhs=q_codes[:].bitcast(FP8X4), rhs_scale=q_scales[:], start=True, stop=True,
             )
-        sg = tile("sg", [P, PACK, Q], F32)
+        sg = tile("sg", [P, PACK, Q], F32, tag="guess_pool")
         for c in range(PACK):
             nc.scalar.activation(
                 sg[:, c, :], score_ps[c // 2][:, c % 2, :], ACT.Sigmoid,
@@ -138,25 +139,23 @@ def tile_attend_answerodds_smoothpage_bymember_pl_kernel(
             )
 
         turn_ps = [bank("d%d" % h, "turn_ps%d" % h, [P, I]) for h in range(QT)]
-        third_ps = bank("b0", "third_ps", [P, I])
-        val_turned = [
-            ps_tile[:, : 2 * P].rearrange("p (u m) -> p u m", u=2) for ps_tile in (turn_ps[0], turn_ps[1], third_ps, turn_ps[0])
-        ]
+        late_ps = bank("b0", "late_ps", [P, 2, 2, P])
+        val_turned = [turn_ps[j][:, : 2 * P].rearrange("p (u m) -> p u m", u=2) for j in range(2)]
+        val_turned.extend(late_ps[:, j] for j in range(2))
 
-        def gather_values(j):
-            picked = tile("val_picked%d" % j, [P, I], BF16, tag=("guess_pool", "val_picked1", "val_picked2", "val_picked3")[j])
-            nc.vector.tensor_copy(picked[:], val_pool[j][:].indirect(slots[:]))
-            return picked
-
-        def turn_values(j, picked):
-            pairs = picked[:].bitcast(F32)
+        def turn_values(j, pairs):
             for u in range(2):
                 nc.tensor.transpose(val_turned[j][:, u, :], pairs[:, u : I // 2 : 2], ident[:])
+
+        def gather_and_turn(j):
+            picked = tile("val_picked%d" % j, [P, I], BF16, tag="val_picked%d" % j if j else "key_scale_pool")
+            nc.vector.tensor_copy(picked[:], val_pool[j][:].indirect(slots[:]))
+            turn_values(j, picked[:].bitcast(F32))
 
         guess_ps = bank("b1", "guess_ps", [P, PACK, P])
         for c in range(PACK):
             nc.tensor.transpose(guess_ps[:, c, :], guess_row[:, c * P : (c + 1) * P], ident[:])
-        turn_values(0, gather_values(0))
+        gather_and_turn(0)
         guess_col = tile("guess_col", [P, PACK], F32)
         rest_col = tile("rest_col", [P, PACK], F32)
         nc.scalar.copy(guess_col[:], guess_ps[:, :, LIVE])
@@ -174,20 +173,15 @@ def tile_attend_answerodds_smoothpage_bymember_pl_kernel(
         v_codes = tile("v_codes", [P, E], U32)
         v_scales = tile("v_scales", [P, E], U8)
 
-        def quantise_values(j, words):
-            cols = slice(j * P, (j + 1) * P)
+        def quantise_values(planes, words):
+            cols = slice(planes.start * P, planes.stop * P)
             nc.vector.quantize_mx(v_codes[:, cols].bitcast(FP8X4), v_scales[:, cols], words.bitcast(BF16))
 
-        def lay_values(j, words, copy):
-            copy(words.rearrange("p (m u) -> p m u", u=2), val_turned[j].rearrange("p u m -> p m u"))
-
-        v_words = [tile("v_words%d" % j, [P, 2 * P], F32)[:] for j in range(PACK - 1)] + [sg[:, PACK - 1, :]]
-        for j in range(1, PACK):
-            lay_values(j - 1, v_words[j - 1], nc.vector.tensor_copy)
-            last_picked = gather_values(j)
-            if j < PACK - 1:
-                turn_values(j, last_picked)
-            quantise_values(j - 1, v_words[j - 1])
+        early_words = tile("early_words", [P, 2, P, 2], F32)
+        for j in range(2):
+            nc.vector.tensor_copy(early_words[:, j], val_turned[j].rearrange("p u m -> p m u"))
+            gather_and_turn(j + 1)
+        quantise_values(range(0, 2), early_words[:].rearrange("p j m u -> p (j m u)"))
 
         neg_lam = tile("neg_lam", [P, QT], F32)
         shares = tile("shares", [P, QT, 2], F32)
@@ -195,10 +189,11 @@ def tile_attend_answerodds_smoothpage_bymember_pl_kernel(
         nc.gpsimd.tensor_scalar(shares[:, :, 0], mix_col[:], -1.0, 1.0, ALU.mult, ALU.add)
         nc.gpsimd.tensor_scalar(shares[:, :, 1], mix_col[:], 1.0 / RUN, 0.0, ALU.mult, ALU.add)
 
-        p, total = [], []
-        stage = tile("stage", [P, PACK + 1, Q], F32)
+        p = []
+        stage = tile("stage", [P, PACK + 2, Q], F32)
         neg_s = stage[:, :PACK, :].rearrange("p t (h s) -> p h t s", h=QT)
-        neg_max = [stage[:, PACK, h : h + 1] for h in range(QT)]
+        total = [stage[:, PACK, h : h + 1] for h in range(QT)]
+        neg_max = [stage[:, PACK + 1, h : h + 1] for h in range(QT)]
         for h in range(QT):
             turned = turn_ps[h]
             for c in range(PACK):
@@ -209,24 +204,20 @@ def tile_attend_answerodds_smoothpage_bymember_pl_kernel(
             )
         for h in range(QT):
             p.append(tile("p%d" % h, [P, PACK, P], F32))
-            total.append(tile("total%d" % h, [P, 1], F32))
-            nc.scalar.activation(p[h][:], neg_s[:, h], ACT.Exp, bias=neg_max[h], scale=-1.0, accum_out=total[h][:])
+            nc.scalar.activation(p[h][:], neg_s[:, h], ACT.Exp, bias=neg_max[h], scale=-1.0, accum_out=total[h])
 
-        turn_values(3, last_picked)
-        lay_values(3, v_words[3], nc.scalar.copy)
-
-        gain = stage[:, PACK, :]
-        member_cols = stage[:, :PACK, :]
-        nc.scalar.activation(gain, gain_pool[:].indirect(picks[:]), ACT.Copy)
-        for j in range(PACK):
-            nc.scalar.activation(member_cols[:, j, :], member_pool[j][:].indirect(picks[:]), ACT.Copy)
+        last_pairs = stage[:, PACK + 1, :]
+        nc.scalar.activation(last_pairs.bitcast(BF16), val_pool[PACK - 1][:].indirect(slots[:]), ACT.Copy)
+        turn_values(PACK - 1, last_pairs)
+        late_words = sg[:, 2:PACK, :]
+        nc.scalar.copy(late_words.rearrange("p j (m u) -> p j m u", u=2), late_ps[:].rearrange("p j u m -> p j m u"))
 
         w_codes, w_scales, w_turned = [], [], []
         for h in range(QT):
+            inv = tile("inv%d" % h, [P, 1], F32)
+            nc.vector.reciprocal(inv[:], total[h])
             run_sum = tile("run_sum%d" % h, [P, G], F32)
             nc.vector.tensor_reduce(run_sum[:], p[h][:].rearrange("p t (g k) -> p g t k", k=2), AX.XY, ALU.add)
-            inv = tile("inv%d" % h, [P, 1], F32)
-            nc.vector.reciprocal(inv[:], total[h][:])
             factor = tile("factor%d" % h, [P, 2], F32)
             nc.vector.tensor_scalar(factor[:], shares[:, h, :], inv[:], None, ALU.mult)
             run_term = tile("run_term%d" % h, [P, G, 2], F32)
@@ -242,7 +233,14 @@ def tile_attend_answerodds_smoothpage_bymember_pl_kernel(
             w_turned.append(bank("a%d" % h, "w_turned%d" % h, [P, PACK, P]))
             for t in range(PACK):
                 nc.tensor.transpose(w_turned[h][:, t, :], w[:, t, :], ident[:])
-        quantise_values(3, v_words[3])
+        quantise_values(range(2, PACK), late_words.rearrange("p j w -> p (j w)"))
+
+        gain = stage[:, PACK, :]
+        member_cols = stage[:, :PACK, :]
+        nc.scalar.activation(gain, gain_pool[:].indirect(picks[:]), ACT.Copy)
+        for j in range(PACK):
+            nc.scalar.activation(member_cols[:, j, :], member_pool[j][:].indirect(picks[:]), ACT.Copy)
+
         for h in range(QT):
             turned = w_turned[h]
             w_bf = tile("w_bf%d" % h, [P, P, PACK], BF16)
@@ -272,7 +270,8 @@ def tile_attend_answerodds_smoothpage_bymember_pl_kernel(
             nc.vector.tensor_tensor(y[:], scaled[:], member_cols[:, :, q_cols], ALU.add)
             nc.sync.dma_start(y_rows[:, :, q_cols], y[:])
             y_bf = tile("y_bf%d" % h, [P, P, PACK], BF16)
-            nc.scalar.copy(y_bf[:], y[:].rearrange("p j q -> p q j"))
+            interleave = nc.vector.tensor_copy if h == QT - 1 else nc.scalar.copy
+            interleave(y_bf[:], y[:].rearrange("p j q -> p q j"))
             nc.vector.quantize_mx(y_codes[:, q_cols].bitcast(FP8X4), y_scales[:, q_cols], y_bf[:].rearrange("p q j -> p (q j)"))
 
         nc.sync.dma_start(out_1[0].rearrange("p c r -> p (c r)").bitcast(I32), y_codes[:].bitcast(I32))

@@ -9,7 +9,8 @@ G = I // RUN
 P = 128
 PACK = 4
 QT = Q // P
-LIVE = 96
+QUADRANT = 32
+LIVE = P - QUADRANT
 
 FLOPS = 2 * D * Q * I + 2 * I * E * Q
 
@@ -71,11 +72,13 @@ def tile_attend_answerodds_smoothpage_bymember_pl_kernel(
         scale_rows = keys_scales[0].bitcast(I32).rearrange("(b r) n -> r b n", r=PACK)
 
         nc.sync.dma_start(slots[:], offs)
+        nc.sync.dma_start(picks[:], offs2)
+        nc.sync.dma_start(os_col[:], slot_factor.rearrange("o (p t) -> p (o t)", t=PACK))
         nc.sync.dma_start(thr_pool[LIVE:P, :], thr[LIVE:P, :])
+        nc.sync.dma_start(steep_pool[LIVE:P, :], steep[LIVE:P, :])
         nc.sync.dma_start(key_pool[:].bitcast(I32), keys_words[0].bitcast(I32))
         for r in range(PACK):
-            nc.sync.dma_start(key_scale_pool[r:P:32, :].bitcast(I32), scale_rows[r])
-        nc.sync.dma_start(steep_pool[LIVE:P, :], steep[LIVE:P, :])
+            nc.sync.dma_start(key_scale_pool[r:P:QUADRANT, :].bitcast(I32), scale_rows[r])
         nc.sync.dma_start(q_raw[:], query.rearrange("(p j) q -> p j q", j=PACK))
         nc.sync.dma_start(guess_pool[LIVE:P, :], guess[LIVE:P, :])
         for j in range(2):
@@ -83,10 +86,8 @@ def tile_attend_answerodds_smoothpage_bymember_pl_kernel(
         with nc.allow_non_contiguous_dma(reason="one factor a query row, one row a partition"):
             nc.sync.dma_start(lam_col[:], lam.rearrange("(h p) o -> p (h o)", p=P))
             nc.sync.dma_start(mix_col[:], mix.rearrange("(h p) o -> p (h o)", p=P))
-        nc.sync.dma_start(val_pool[2][:], val_planes[2])
-        nc.sync.dma_start(os_col[:], slot_factor.rearrange("o (p t) -> p (o t)", t=PACK))
-        nc.sync.dma_start(picks[:], offs2)
-        nc.sync.dma_start(val_pool[3][:], val_planes[3])
+        for j in range(2, PACK):
+            nc.sync.dma_start(val_pool[j][:], val_planes[j])
         nc.sync.dma_start(gain_pool[:], mgain)
         for j in range(PACK):
             nc.sync.dma_start(member_pool[j][:], member_planes[j])
@@ -109,9 +110,9 @@ def tile_attend_answerodds_smoothpage_bymember_pl_kernel(
         nc.scalar.activation(steep_row[:], steep_pool[:].indirect(slots[:]), ACT.Copy)
         thr_ps = bank("c0", "thr_ps", [P, PACK, P])
         steep_ps = bank("c1", "steep_ps", [P, PACK, P])
-        for row, turned in ((thr_row, thr_ps), (steep_row, steep_ps)):
+        for row, row_ps in ((thr_row, thr_ps), (steep_row, steep_ps)):
             for c in range(PACK):
-                nc.tensor.transpose(turned[:, c, :], row[:, c * P : (c + 1) * P], ident[:])
+                nc.tensor.transpose(row_ps[:, c, :], row[:, c * P : (c + 1) * P], ident[:])
         steep_col = tile("steep_col", [P, PACK], F32)
         shift_col = tile("shift_col", [P, PACK], F32)
         nc.scalar.copy(steep_col[:], steep_ps[:, :, LIVE])
@@ -119,11 +120,9 @@ def tile_attend_answerodds_smoothpage_bymember_pl_kernel(
             nc.scalar.activation(
                 shift_col[:, c : c + 1], thr_ps[:, c, LIVE : LIVE + 1], ACT.Copy, scale=steep_col[:, c : c + 1]
             )
-
-
         nc.scalar.activation(guess_row[:], guess_pool[:].indirect(slots[:]), ACT.Copy)
 
-        score_ps = [bank("a%d" % h, "score_ps%d" % h, [P, 2, Q]) for h in range(2)]
+        score_ps = [bank("a%d" % b, "score_ps%d" % b, [P, 2, Q]) for b in range(PACK // 2)]
         for c in range(PACK):
             cols = slice(c * P, (c + 1) * P)
             nc.tensor.matmul_mx(
@@ -170,6 +169,7 @@ def tile_attend_answerodds_smoothpage_bymember_pl_kernel(
 
         warm_out2 = tile("warm_out2", [P, 1], F32)
         nc.scalar.activation(warm_out2[:], log_chance[:, PACK - 1, 0:1], ACT.Exp)
+
         v_codes = tile("v_codes", [P, E], U32)
         v_scales = tile("v_scales", [P, E], U8)
 
@@ -195,11 +195,10 @@ def tile_attend_answerodds_smoothpage_bymember_pl_kernel(
         total = [stage[:, PACK, h : h + 1] for h in range(QT)]
         neg_max = [stage[:, PACK + 1, h : h + 1] for h in range(QT)]
         for h in range(QT):
-            turned = turn_ps[h]
             for c in range(PACK):
-                nc.tensor.transpose(turned[:, c * P : (c + 1) * P], log_chance[:, c, h * P : (h + 1) * P], ident[:])
+                nc.tensor.transpose(turn_ps[h][:, c * P : (c + 1) * P], log_chance[:, c, h * P : (h + 1) * P], ident[:])
             nc.vector.tensor_scalar(
-                neg_s[:, h], turned[:].rearrange("p (s t) -> p t s", t=PACK), neg_lam[:, h : h + 1], None,
+                neg_s[:, h], turn_ps[h][:].rearrange("p (s t) -> p t s", t=PACK), neg_lam[:, h : h + 1], None,
                 ALU.mult, ALU.min, accum_out=neg_max[h],
             )
         for h in range(QT):
@@ -242,10 +241,9 @@ def tile_attend_answerodds_smoothpage_bymember_pl_kernel(
             nc.scalar.activation(member_cols[:, j, :], member_pool[j][:].indirect(picks[:]), ACT.Copy)
 
         for h in range(QT):
-            turned = w_turned[h]
             w_bf = tile("w_bf%d" % h, [P, P, PACK], BF16)
             nc.vector.tensor_tensor(
-                w_bf[:], turned[:].rearrange("p t q -> p q t"),
+                w_bf[:], w_turned[h][:].rearrange("p t q -> p q t"),
                 os_col[:].unsqueeze(1).broadcast_to([P, P, PACK]), ALU.mult,
             )
             w_codes.append(tile("w_codes%d" % h, [P, P], U32))
@@ -278,4 +276,4 @@ def tile_attend_answerodds_smoothpage_bymember_pl_kernel(
         out_scale_rows = out_2[0].bitcast(I32).rearrange("(b r) n -> r b n", r=PACK)
         for r in range(PACK):
             queue = nc.scalar if r % 2 else nc.sync
-            queue.dma_start(out_scale_rows[r], y_scales[r:P:32, :].bitcast(I32))
+            queue.dma_start(out_scale_rows[r], y_scales[r:P:QUADRANT, :].bitcast(I32))

from contextlib import ExitStack

import concourse.mybir as mybir
from concourse.masks import make_identity

D, T, I, Q, E, M = 512, 2048, 512, 256, 512, 1024
RUN = 8
G = I // RUN
P = 128
PACK = 4
QT = Q // P
QUADRANT = 32
LIVE = P - QUADRANT

FLOPS = 2 * D * Q * I + 2 * I * E * Q

F32 = mybir.dt.float32
BF16 = mybir.dt.bfloat16
I32 = mybir.dt.int32
U32 = mybir.dt.uint32
U16 = mybir.dt.uint16
U8 = mybir.dt.uint8
FP8X4 = mybir.dt.float8_e4m3fn_x4
FP4X4 = mybir.dt.float4_e2m1fn_x4
ALU = mybir.AluOpType
ACT = mybir.ActivationFunctionType
AX = mybir.AxisListType


def tile_attend_answerodds_smoothpage_bymember_pl_kernel(
    tc, query, keys_words, keys_scales, guess, steep, thr, lam, mix, slot_factor, vals, member, mgain, offs, offs2,
    out_0, out_1, out_2,
):
    nc = tc.nc
    with ExitStack() as ctx:
        sb = ctx.enter_context(tc.tile_pool(name="sb", bufs=1))
        ps = ctx.enter_context(tc.psum_pool(name="ps", bufs=1))

        def tile(name, shape, dtype, tag=""):
            return sb.tile(shape, dtype, name=name, tag=tag or name, align_bytes=64)

        def bank(tag, name, shape):
            return ps.tile(shape, F32, name=name, tag=tag)

        slots = tile("slots", [P, I // 16], U16)
        picks = tile("picks", [P, Q // 16], U16)
        key_pool = tile("key_pool", [P, T], U16)
        key_scale_pool = tile("key_scale_pool", [P, T], U8)
        thr_pool = tile("thr_pool", [P, T], F32)
        steep_pool = tile("steep_pool", [P, T], F32)
        guess_pool = tile("guess_pool", [P, T], F32)
        q_raw = tile("q_raw", [P, PACK, Q], F32)
        val_pool = [tile("val_pool%d" % j, [P, T], F32) for j in range(PACK)]
        member_pool = [tile("member_pool%d" % j, [P, M], F32) for j in range(PACK)]
        gain_pool = tile("gain_pool", [P, M], F32)
        lam_col = tile("lam_col", [P, QT], F32)
        mix_col = tile("mix_col", [P, QT], F32)
        os_col = tile("os_col", [P, PACK], F32)
        ident = tile("ident", [P, P], F32)

        nc.gpsimd.memset(key_scale_pool[:].bitcast(I32), 0)
        warm_in = tile("warm_in", [P, 1], F32)
        warm_out = tile("warm_out", [P, 1], F32)
        nc.gpsimd.memset(warm_in[:], 0.0)
        nc.scalar.activation(warm_out[:], warm_in[:], ACT.Sigmoid)
        make_identity(nc, ident[:])
        for pool in (thr_pool, steep_pool, guess_pool):
            nc.vector.memset(pool[0:LIVE, :], 0.0)

        val_planes = vals.rearrange("(m j) t -> j m t", j=PACK)
        member_planes = member.rearrange("(m j) n -> j m n", j=PACK)
        scale_rows = keys_scales[0].bitcast(I32).rearrange("(b r) n -> r b n", r=PACK)

        nc.sync.dma_start(slots[:], offs)
        nc.sync.dma_start(picks[:], offs2)
        nc.sync.dma_start(os_col[:], slot_factor.rearrange("o (p t) -> p (o t)", t=PACK))
        nc.sync.dma_start(thr_pool[LIVE:P, :], thr[LIVE:P, :])
        nc.sync.dma_start(steep_pool[LIVE:P, :], steep[LIVE:P, :])
        nc.sync.dma_start(key_pool[:].bitcast(I32), keys_words[0].bitcast(I32))
        for r in range(PACK):
            nc.sync.dma_start(key_scale_pool[r:P:QUADRANT, :].bitcast(I32), scale_rows[r])
        nc.sync.dma_start(q_raw[:], query.rearrange("(p j) q -> p j q", j=PACK))
        nc.sync.dma_start(guess_pool[LIVE:P, :], guess[LIVE:P, :])
        for j in range(2):
            nc.sync.dma_start(val_pool[j][:], val_planes[j])
        with nc.allow_non_contiguous_dma(reason="one factor a query row, one row a partition"):
            nc.sync.dma_start(lam_col[:], lam.rearrange("(h p) o -> p (h o)", p=P))
            nc.sync.dma_start(mix_col[:], mix.rearrange("(h p) o -> p (h o)", p=P))
        for j in range(2, PACK):
            nc.sync.dma_start(val_pool[j][:], val_planes[j])
        nc.sync.dma_start(gain_pool[:], mgain)
        for j in range(PACK):
            nc.sync.dma_start(member_pool[j][:], member_planes[j])

        key_words = tile("key_words", [P, I], U16)
        key_scales = tile("key_scales", [P, I], U8)
        nc.vector.tensor_copy(key_words[:], key_pool[:].indirect(slots[:]))
        nc.vector.tensor_copy(key_scales[:], key_scale_pool[:].indirect(slots[:]))

        q_bf = tile("q_bf", [P, Q, PACK], BF16)
        q_codes = tile("q_codes", [P, Q], U32)
        q_scales = tile("q_scales", [P, Q], U8)
        nc.vector.tensor_copy(q_bf[:], q_raw[:].rearrange("p j q -> p q j"))
        nc.vector.quantize_mx(q_codes[:].bitcast(FP8X4), q_scales[:], q_bf[:].rearrange("p q j -> p (q j)"))

        thr_row = tile("thr_row", [P, I], F32)
        steep_row = tile("steep_row", [P, I], F32)
        guess_row = tile("guess_row", [P, I], F32)
        nc.scalar.activation(thr_row[:], thr_pool[:].indirect(slots[:]), ACT.Copy, scale=-1.0)
        nc.scalar.activation(steep_row[:], steep_pool[:].indirect(slots[:]), ACT.Copy)
        thr_ps = bank("c0", "thr_ps", [P, PACK, P])
        steep_ps = bank("c1", "steep_ps", [P, PACK, P])
        for row, row_ps in ((thr_row, thr_ps), (steep_row, steep_ps)):
            for c in range(PACK):
                nc.tensor.transpose(row_ps[:, c, :], row[:, c * P : (c + 1) * P], ident[:])
        steep_col = tile("steep_col", [P, PACK], F32)
        shift_col = tile("shift_col", [P, PACK], F32)
        nc.scalar.copy(steep_col[:], steep_ps[:, :, LIVE])
        for c in range(PACK):
            nc.scalar.activation(
                shift_col[:, c : c + 1], thr_ps[:, c, LIVE : LIVE + 1], ACT.Copy, scale=steep_col[:, c : c + 1]
            )
        nc.scalar.activation(guess_row[:], guess_pool[:].indirect(slots[:]), ACT.Copy)

        score_ps = [bank("a%d" % b, "score_ps%d" % b, [P, 2, Q]) for b in range(PACK // 2)]
        for c in range(PACK):
            cols = slice(c * P, (c + 1) * P)
            nc.tensor.matmul_mx(
                score_ps[c // 2][:, c % 2, :],
                lhsT=key_words[:, cols].bitcast(FP4X4), lhsT_scale=key_scales[:, cols],
                rhs=q_codes[:].bitcast(FP8X4), rhs_scale=q_scales[:], start=True, stop=True,
            )
        sg = tile("sg", [P, PACK, Q], F32, tag="guess_pool")
        for c in range(PACK):
            nc.scalar.activation(
                sg[:, c, :], score_ps[c // 2][:, c % 2, :], ACT.Sigmoid,
                bias=shift_col[:, c : c + 1], scale=steep_col[:, c : c + 1],
            )

        turn_ps = [bank("d%d" % h, "turn_ps%d" % h, [P, I]) for h in range(QT)]
        late_ps = bank("b0", "late_ps", [P, 2, 2, P])
        val_turned = [turn_ps[j][:, : 2 * P].rearrange("p (u m) -> p u m", u=2) for j in range(2)]
        val_turned.extend(late_ps[:, j] for j in range(2))

        def turn_values(j, pairs):
            for u in range(2):
                nc.tensor.transpose(val_turned[j][:, u, :], pairs[:, u : I // 2 : 2], ident[:])

        def gather_and_turn(j):
            picked = tile("val_picked%d" % j, [P, I], BF16, tag="val_picked%d" % j if j else "key_scale_pool")
            nc.vector.tensor_copy(picked[:], val_pool[j][:].indirect(slots[:]))
            turn_values(j, picked[:].bitcast(F32))

        guess_ps = bank("b1", "guess_ps", [P, PACK, P])
        for c in range(PACK):
            nc.tensor.transpose(guess_ps[:, c, :], guess_row[:, c * P : (c + 1) * P], ident[:])
        gather_and_turn(0)
        guess_col = tile("guess_col", [P, PACK], F32)
        rest_col = tile("rest_col", [P, PACK], F32)
        nc.scalar.copy(guess_col[:], guess_ps[:, :, LIVE])
        nc.scalar.activation(rest_col[:], guess_ps[:, :, LIVE], ACT.Copy, bias=1.0, scale=-1.0)

        log_chance = tile("log_chance", [P, PACK, Q], F32)
        for c in range(PACK):
            nc.scalar.activation(
                log_chance[:, c, :], sg[:, c, :], ACT.Ln,
                bias=guess_col[:, c : c + 1], scale=rest_col[:, c : c + 1],
            )

        warm_out2 = tile("warm_out2", [P, 1], F32)
        nc.scalar.activation(warm_out2[:], log_chance[:, PACK - 1, 0:1], ACT.Exp)

        v_codes = tile("v_codes", [P, E], U32)
        v_scales = tile("v_scales", [P, E], U8)

        def quantise_values(planes, words):
            cols = slice(planes.start * P, planes.stop * P)
            nc.vector.quantize_mx(v_codes[:, cols].bitcast(FP8X4), v_scales[:, cols], words.bitcast(BF16))

        early_words = tile("early_words", [P, 2, P, 2], F32)
        for j in range(2):
            nc.vector.tensor_copy(early_words[:, j], val_turned[j].rearrange("p u m -> p m u"))
            gather_and_turn(j + 1)
        quantise_values(range(0, 2), early_words[:].rearrange("p j m u -> p (j m u)"))

        neg_lam = tile("neg_lam", [P, QT], F32)
        shares = tile("shares", [P, QT, 2], F32)
        nc.gpsimd.tensor_scalar(neg_lam[:], lam_col[:], -1.0, 0.0, ALU.mult, ALU.add)
        nc.gpsimd.tensor_scalar(shares[:, :, 0], mix_col[:], -1.0, 1.0, ALU.mult, ALU.add)
        nc.gpsimd.tensor_scalar(shares[:, :, 1], mix_col[:], 1.0 / RUN, 0.0, ALU.mult, ALU.add)

        p = []
        stage = tile("stage", [P, PACK + 2, Q], F32)
        neg_s = stage[:, :PACK, :].rearrange("p t (h s) -> p h t s", h=QT)
        total = [stage[:, PACK, h : h + 1] for h in range(QT)]
        neg_max = [stage[:, PACK + 1, h : h + 1] for h in range(QT)]
        for h in range(QT):
            for c in range(PACK):
                nc.tensor.transpose(turn_ps[h][:, c * P : (c + 1) * P], log_chance[:, c, h * P : (h + 1) * P], ident[:])
            nc.vector.tensor_scalar(
                neg_s[:, h], turn_ps[h][:].rearrange("p (s t) -> p t s", t=PACK), neg_lam[:, h : h + 1], None,
                ALU.mult, ALU.min, accum_out=neg_max[h],
            )
        for h in range(QT):
            p.append(tile("p%d" % h, [P, PACK, P], F32))
            nc.scalar.activation(p[h][:], neg_s[:, h], ACT.Exp, bias=neg_max[h], scale=-1.0, accum_out=total[h])

        last_pairs = stage[:, PACK + 1, :]
        nc.scalar.activation(last_pairs.bitcast(BF16), val_pool[PACK - 1][:].indirect(slots[:]), ACT.Copy)
        turn_values(PACK - 1, last_pairs)
        late_words = sg[:, 2:PACK, :]
        nc.scalar.copy(late_words.rearrange("p j (m u) -> p j m u", u=2), late_ps[:].rearrange("p j u m -> p j m u"))

        w_codes, w_scales, w_turned = [], [], []
        for h in range(QT):
            inv = tile("inv%d" % h, [P, 1], F32)
            nc.vector.reciprocal(inv[:], total[h])
            run_sum = tile("run_sum%d" % h, [P, G], F32)
            nc.vector.tensor_reduce(run_sum[:], p[h][:].rearrange("p t (g k) -> p g t k", k=2), AX.XY, ALU.add)
            factor = tile("factor%d" % h, [P, 2], F32)
            nc.vector.tensor_scalar(factor[:], shares[:, h, :], inv[:], None, ALU.mult)
            run_term = tile("run_term%d" % h, [P, G, 2], F32)
            nc.vector.tensor_scalar(
                run_term[:], run_sum[:].unsqueeze(2).broadcast_to([P, G, 2]), factor[:, 1:2], None, ALU.mult
            )
            w = tile("w%d" % h, [P, PACK, P], F32)
            nc.vector.scalar_tensor_tensor(
                w[:], p[h][:], factor[:, 0:1],
                run_term[:].rearrange("p g k -> p (g k)").unsqueeze(1).broadcast_to([P, PACK, P]),
                ALU.mult, ALU.add,
            )
            w_turned.append(bank("a%d" % h, "w_turned%d" % h, [P, PACK, P]))
            for t in range(PACK):
                nc.tensor.transpose(w_turned[h][:, t, :], w[:, t, :], ident[:])
        quantise_values(range(2, PACK), late_words.rearrange("p j w -> p (j w)"))

        gain = stage[:, PACK, :]
        member_cols = stage[:, :PACK, :]
        nc.scalar.activation(gain, gain_pool[:].indirect(picks[:]), ACT.Copy)
        for j in range(PACK):
            nc.scalar.activation(member_cols[:, j, :], member_pool[j][:].indirect(picks[:]), ACT.Copy)

        for h in range(QT):
            w_bf = tile("w_bf%d" % h, [P, P, PACK], BF16)
            nc.vector.tensor_tensor(
                w_bf[:], w_turned[h][:].rearrange("p t q -> p q t"),
                os_col[:].unsqueeze(1).broadcast_to([P, P, PACK]), ALU.mult,
            )
            w_codes.append(tile("w_codes%d" % h, [P, P], U32))
            w_scales.append(tile("w_scales%d" % h, [P, P], U8))
            nc.vector.quantize_mx(w_codes[h][:].bitcast(FP8X4), w_scales[h][:], w_bf[:].rearrange("p q t -> p (q t)"))

        y_codes = tile("y_codes", [P, Q], U32)
        y_scales = tile("y_scales", [P, Q], U8)
        y_rows = out_0.rearrange("(m j) q -> m j q", j=PACK)
        for h in range(QT):
            q_cols = slice(h * P, (h + 1) * P)
            o_ps = bank("c%d" % h, "o_ps%d" % h, [P, PACK, P])
            for j in range(PACK):
                cols = slice(j * P, (j + 1) * P)
                nc.tensor.matmul_mx(
                    o_ps[:, j, :], lhsT=v_codes[:, cols].bitcast(FP8X4), lhsT_scale=v_scales[:, cols],
                    rhs=w_codes[h][:].bitcast(FP8X4), rhs_scale=w_scales[h][:], start=True, stop=True,
                )
            scaled = tile("scaled%d" % h, [P, PACK, P], F32)
            nc.vector.tensor_tensor(scaled[:], o_ps[:], gain[:, q_cols].unsqueeze(1).broadcast_to([P, PACK, P]), ALU.mult)
            y = tile("y%d" % h, [P, PACK, P], F32)
            nc.vector.tensor_tensor(y[:], scaled[:], member_cols[:, :, q_cols], ALU.add)
            nc.sync.dma_start(y_rows[:, :, q_cols], y[:])
            y_bf = tile("y_bf%d" % h, [P, P, PACK], BF16)
            interleave = nc.vector.tensor_copy if h == QT - 1 else nc.scalar.copy
            interleave(y_bf[:], y[:].rearrange("p j q -> p q j"))
            nc.vector.quantize_mx(y_codes[:, q_cols].bitcast(FP8X4), y_scales[:, q_cols], y_bf[:].rearrange("p q j -> p (q j)"))

        nc.sync.dma_start(out_1[0].rearrange("p c r -> p (c r)").bitcast(I32), y_codes[:].bitcast(I32))
        out_scale_rows = out_2[0].bitcast(I32).rearrange("(b r) n -> r b n", r=PACK)
        for r in range(PACK):
            queue = nc.scalar if r % 2 else nc.sync
            queue.dma_start(out_scale_rows[r], y_scales[r:P:QUADRANT, :].bitcast(I32))
